import numpy as np
import ml_dtypes


def mxq(x, axis, fmt="e4m3"):
    dtype, down = {"e4m3": (ml_dtypes.float8_e4m3fn, 7), "e5m2": (ml_dtypes.float8_e5m2, 14)}[fmt]
    v = np.moveaxis(np.asarray(x, np.float32).astype(ml_dtypes.bfloat16).astype(np.float64), axis, -1)
    blocks = v.reshape(v.shape[:-1] + (-1, 32))
    amax = np.abs(blocks).max(-1, keepdims=True)
    byte = np.maximum(np.where(amax > 0, np.frexp(amax)[1] - 1 + 127, 0) - down, 1)
    scale = np.exp2(byte - 127.0)
    codes = (blocks / scale).astype(np.float32).astype(dtype).astype(np.float64)
    return np.moveaxis((codes * scale).reshape(v.shape), -1, axis)


WIDE = False


def mx_kscale(k):
    if not WIDE:
        return np.ones(k)
    levels = np.array([10, -10, 5, -5, 0])
    if k % 512:
        return np.exp2(np.random.permutation(np.resize(levels, k // 32))).repeat(32)
    a = np.empty((k // 512, 16))
    for p in range(k // 512):
        a[p, :8] = np.random.permutation(np.resize(levels, 8))
        for g in range(8):
            far = levels[np.abs(levels - a[p, g]) >= 10]
            a[p, g + 8] = far[np.random.randint(len(far))]
    return np.exp2(a.ravel()).repeat(32)


def f64(x):
    return np.asarray(x).astype(np.float64)


def striped(idx):
    return np.tile(np.asarray(idx).reshape(-1, 16).T, (8, 1)).astype(np.uint16)


def unstriped(offs):
    return offs[:16].T.reshape(-1).astype(np.int64)


E2M1 = np.array([0.0, 0.5, 1.0, 1.5, 2.0, 3.0, 4.0, 6.0, -0.0, -0.5, -1.0, -1.5, -2.0, -3.0, -4.0, -6.0])


def pack_weight(w, fmt):
    k, n = w.shape
    w = f64(np.asarray(w, np.float32).astype(ml_dtypes.bfloat16)).reshape(k // 32, 32, n)
    amax = np.abs(w).max(1)
    if fmt == "e4m3":
        byte = np.frexp(amax)[1] - 1 + 127 - 7
    else:
        mant, ex = np.frexp(amax / 6.0)
        byte = np.where(mant > 0.5, ex, ex - 1) + 127
    byte = np.clip(np.where(amax > 0, byte, 1), 1, 254)
    scaled = (w * np.exp2(127.0 - byte)[:, None, :]).reshape(k, n).astype(np.float32)
    by_word = np.ascontiguousarray(scaled.reshape(k // 512, 128, 4, n).transpose(0, 1, 3, 2))
    if fmt == "e4m3":
        words = by_word.astype(ml_dtypes.float8_e4m3fn).view(np.uint8)
    else:
        c = by_word.astype(ml_dtypes.float4_e2m1fn).view(np.uint8) & 0xF
        words = (c[..., 0::2] | (c[..., 1::2] << 4)).reshape(k // 512, 128, 2 * n)
    return np.ascontiguousarray(words), np.ascontiguousarray(byte.astype(np.uint8).reshape(k // 512, 16, n))


def unpack_weight(words, scales, fmt):
    g, _, n = scales.shape
    words = np.ascontiguousarray(words).reshape(g, 128, n, -1)
    if fmt == "e4m3":
        vals = words.view(ml_dtypes.float8_e4m3fn).astype(np.float64)
    else:
        nib = np.empty((g, 128, n, 4), np.uint8)
        nib[..., 0::2] = words & 0xF
        nib[..., 1::2] = words >> 4
        vals = E2M1[nib]
    vals = vals * np.repeat(np.exp2(scales.astype(np.float64) - 127.0), 8, axis=1)[..., None]
    return vals.transpose(0, 1, 3, 2).reshape(g * 512, n)


def bf(x):
    return np.asarray(x, np.float32).astype(ml_dtypes.bfloat16)


def planes(Y):
    r, m = Y.shape
    b = f64(bf(Y)).reshape(r // 32, 32, m)
    amax = np.abs(b).max(1)
    byte = np.clip(np.where(amax > 0, np.frexp(amax)[1] - 1 + 127 - 7, 1), 1, 254)
    codes = (b * np.exp2(127.0 - byte)[:, None, :]).reshape(r, m).astype(np.float32).astype(ml_dtypes.float8_e4m3fn).view(np.uint8)
    words = codes.reshape(r // 512, 128, 4, m).transpose(0, 1, 3, 2)
    return np.ascontiguousarray(words), np.ascontiguousarray(byte.astype(np.uint8).reshape(r // 512, 16, m))


K, T, J, B, R, N = 512, 1024, 512, 64, 512, 512


def setup_inputs():
    n = np.random.standard_normal
    idx = (np.random.permutation(T // 8)[:J // 8, None] * 8 + np.arange(8)).reshape(-1)
    fk = mx_kscale(K)
    fr = mx_kscale(R)
    xtp = pack_weight(n((K, T)) / fk[:, None], "e2m1")
    wap = pack_weight(n((K, R)) * 1 / np.sqrt(K) * fk[:, None] * fr, "e4m3")
    wbp = pack_weight(n((R, N)) * 1 / np.sqrt(R) / fr[:, None], "e2m1")
    return {
        "xt_words": xtp[0],
        "xt_scales": xtp[1],
        "wa_words": wap[0],
        "wa_scales": wap[1],
        "wb_words": wbp[0],
        "wb_scales": wbp[1],
        "res": (1.0 * n((N, T))).astype(np.float32),
        "offs": striped(idx),
    }


def reference(xt_words, xt_scales, wa_words, wa_scales, wb_words, wb_scales, res, offs):
    idx = unstriped(offs)
    xtu = unpack_weight(xt_words, xt_scales, "e2m1")
    wau = unpack_weight(wa_words, wa_scales, "e4m3")
    wbu = unpack_weight(wb_words, wb_scales, "e2m1")
    xtidxg = xtu[:, idx]
    a = wau.T @ xtidxg
    m1 = a.reshape(R, B, J // B).mean(axis=2)
    mr = np.repeat(m1, J // B, axis=1)
    hid = np.maximum(a - mr, 0.0)
    hidq = mxq(hid, 0, "e4m3")
    p = wbu.T @ hidq
    pg = np.zeros((N, T))
    pg[:, idx] = p
    y = pg + 0.2 * f64(res)
    words, scales = planes(y)
    return y, words, scales

@@ -1,0 +1,234 @@
+from contextlib import ExitStack
+
+import concourse.mybir as mybir
+
+K, T, J, R, N = 512, 1024, 512, 512, 512
+FLOPS = 2 * K * R * J + 2 * R * N * J
+
+F32 = mybir.dt.float32
+BF16 = mybir.dt.bfloat16
+I32 = mybir.dt.int32
+U32 = mybir.dt.uint32
+U16 = mybir.dt.uint16
+U8 = mybir.dt.uint8
+FP8X4 = mybir.dt.float8_e4m3fn_x4
+FP4X4 = mybir.dt.float4_e2m1fn_x4
+ALU = mybir.AluOpType
+ACT = mybir.ActivationFunctionType
+AXIS_X = mybir.AxisListType.X
+
+P = 128
+PACK = 4
+RUN = 8
+CHUNK = 128
+HALF = 256
+OUT_CHUNK = 256
+
+
+def load_scale_rows(nc, plane, rows):
+    for q in range(4):
+        nc.sync.dma_start(out=plane[32 * q : 32 * q + 4, :].bitcast(I32), in_=rows[4 * q : 4 * q + 4, :].bitcast(I32))
+
+
+def tile_moe_expert_hidden_less_block_mean_pl_kernel(
+    tc, xt_words, xt_scales, wa_words, wa_scales, wb_words, wb_scales, res, offs, out_0, out_1, out_2
+):
+    nc = tc.nc
+    with ExitStack() as ctx:
+        keep = ctx.enter_context(tc.tile_pool(name="keep", bufs=1))
+        psum = ctx.enter_context(tc.psum_pool(name="psum", bufs=1))
+
+        offsets = keep.tile([P, J // 16], U16, name="offsets")
+        nc.sync.dma_start(offsets[:], offs)
+
+        x_scale_raw = keep.tile([P, T], U8, name="x_scale_raw", align_bytes=64)
+        wa_scale_raw = keep.tile([P, R], U8, name="wa_scale_raw", align_bytes=64)
+        wb_scale_raw = keep.tile([P, N], U8, name="wb_scale_raw", align_bytes=64)
+        nc.vector.memset(x_scale_raw[:].bitcast(I32), 0)
+        nc.vector.memset(wa_scale_raw[:].bitcast(I32), 0)
+        nc.vector.memset(wb_scale_raw[:].bitcast(I32), 0)
+        placed = [keep.tile([P, T], F32, name=f"placed{u}", align_bytes=64) for u in range(2)]
+        for u in range(2):
+            nc.vector.memset(placed[u][:], 0.0)
+
+        x_raw = keep.tile([P, 2 * T], U8, name="x_raw", align_bytes=64)
+        wa_raw = keep.tile([P, R], I32, name="wa_raw", align_bytes=64)
+        wb_raw = keep.tile([P, 2 * N], U8, name="wb_raw", align_bytes=64)
+        nc.sync.dma_start(out=x_raw[:].bitcast(I32), in_=xt_words[0].bitcast(I32))
+        load_scale_rows(nc, x_scale_raw, xt_scales[0])
+        nc.sync.dma_start(out=wa_raw[:], in_=wa_words[0].rearrange("p c r -> p (c r)").bitcast(I32))
+        load_scale_rows(nc, wa_scale_raw, wa_scales[0])
+        nc.sync.dma_start(out=wb_raw[:].bitcast(I32), in_=wb_words[0].bitcast(I32))
+        load_scale_rows(nc, wb_scale_raw, wb_scales[0])
+        res_rows = res.rearrange("(p t) c -> p t c", t=PACK)
+        res_sb = [keep.tile([P, T], F32, name=f"res{t}") for t in range(PACK)]
+        for t in range(PACK):
+            nc.sync.dma_start(out=res_sb[t][:], in_=res_rows[:, t, :])
+
+        x_words = keep.tile([P, 2 * J], U8, name="x_words", align_bytes=64)
+        x_scales = keep.tile([P, J], U8, name="x_scales", align_bytes=64)
+        wa_dealt = keep.tile([P, R], I32, name="wa_dealt", align_bytes=64)
+        wa_scale = keep.tile([P, R], U8, name="wa_scale", align_bytes=64)
+        wb_dealt = keep.tile([P, 2 * N], U8, name="wb_dealt", align_bytes=64)
+        wb_scale = keep.tile([P, N], U8, name="wb_scale", align_bytes=64)
+
+        def gather(h):
+            cols = slice(h * HALF, (h + 1) * HALF)
+            listed = offsets[:, h * HALF // 16 : (h + 1) * HALF // 16]
+            nc.vector.tensor_copy(x_words[:].bitcast(U16)[:, cols], x_raw[:].bitcast(U16).indirect(listed))
+            nc.vector.tensor_copy(x_scales[:, cols], x_scale_raw[:].indirect(listed))
+
+        def deal(dst, src):
+            nc.vector.tensor_copy(
+                out=dst.rearrange("p (t m) -> p m t", t=PACK), in_=src.rearrange("p (m t) -> p m t", t=PACK)
+            )
+
+        banks = [psum.tile([P, PACK, CHUNK], F32, name=f"a_bank{c}") for c in range(J // CHUNK)]
+        sums = [keep.tile([P, PACK, CHUNK // RUN], F32, name=f"sums{c}") for c in range(J // CHUNK)]
+        means = [keep.tile([P, CHUNK // RUN, PACK], F32, name=f"means{c}") for c in range(J // CHUNK)]
+        centred = keep.tile([P, J * PACK], BF16, name="centred", align_bytes=64)
+        hid = keep.tile([P, J * PACK], BF16, name="hid", align_bytes=64)
+        hid_codes = keep.tile([P, J], U32, name="hid_codes", align_bytes=64)
+        hid_scales = keep.tile([P, J], U8, name="hid_scales", align_bytes=64)
+
+        def first_layer(c):
+            cols = slice(c * CHUNK, (c + 1) * CHUNK)
+            for t in range(PACK):
+                w_cols = slice(t * P, (t + 1) * P)
+                nc.tensor.matmul_mx(
+                    out=banks[c][:, t, :],
+                    lhsT=wa_dealt[:, w_cols].bitcast(FP8X4),
+                    lhsT_scale=wa_scale[:, w_cols],
+                    rhs=x_words[:, 2 * c * CHUNK : 2 * (c + 1) * CHUNK].bitcast(FP4X4),
+                    rhs_scale=x_scales[:, cols],
+                    start=True,
+                    stop=True,
+                )
+
+        def block_means(c):
+            nc.vector.tensor_reduce(
+                out=sums[c][:].rearrange("p t b -> p (t b)"),
+                in_=banks[c][:].rearrange("p t (b i) -> p (t b) i", i=RUN),
+                axis=AXIS_X,
+                op=ALU.add,
+            )
+            nc.scalar.activation(
+                out=means[c][:], in_=sums[c][:].rearrange("p t b -> p b t"), func=ACT.Copy, scale=1.0 / RUN
+            )
+
+        def centre(c):
+            cols = slice(c * CHUNK * PACK, (c + 1) * CHUNK * PACK)
+            nc.vector.tensor_tensor(
+                out=centred[:, cols].rearrange("p (b i t) -> p b i t", i=RUN, t=PACK),
+                in0=banks[c][:].rearrange("p t (b i) -> p b i t", i=RUN),
+                in1=means[c][:].rearrange("p b (o t) -> p b o t", o=1).to_broadcast([P, CHUNK // RUN, RUN, PACK]),
+                op=ALU.subtract,
+            )
+            nc.scalar.activation(out=hid[:, cols], in_=centred[:, cols], func=ACT.Relu)
+
+        def quantize_hidden(h):
+            cols = slice(h * HALF, (h + 1) * HALF)
+            nc.vector.quantize_mx(
+                out=hid_codes[:, cols].bitcast(FP8X4),
+                scales=hid_scales[:, cols],
+                in_=hid[:, h * HALF * PACK : (h + 1) * HALF * PACK],
+            )
+
+        p_banks = [[psum.tile([P, 2, HALF], F32, name=f"p_bank{h}{u}") for u in range(2)] for h in range(2)]
+        p_sb = [keep.tile([P, 2, J], F32, name=f"p_sb{u}") for u in range(2)]
+
+        def second_layer(h):
+            cols = slice(h * HALF, (h + 1) * HALF)
+            for u in range(2):
+                for e in range(2):
+                    t = 2 * u + e
+                    nc.tensor.matmul_mx(
+                        out=p_banks[h][u][:, e, :],
+                        lhsT=wb_dealt[:, 2 * t * P : 2 * (t + 1) * P].bitcast(FP4X4),
+                        lhsT_scale=wb_scale[:, t * P : (t + 1) * P],
+                        rhs=hid_codes[:, cols].bitcast(FP8X4),
+                        rhs_scale=hid_scales[:, cols],
+                        start=True,
+                        stop=True,
+                    )
+                nc.scalar.copy(out=p_sb[u][:, :, cols], in_=p_banks[h][u][:])
+
+        def scatter(t, lo, hi):
+            nc.vector.tensor_copy(
+                placed[t % 2][:].indirect(offsets[:, lo // 16 : hi // 16]), p_sb[t // 2][:, t % 2, lo:hi]
+            )
+
+        y = keep.tile([P, PACK, T], F32, name="y")
+        out_rows = out_0.rearrange("(p t) c -> p t c", t=PACK)
+
+        def add_residual(t, lo, hi):
+            nc.vector.scalar_tensor_tensor(
+                out=y[:, t, lo:hi], in0=res_sb[t][:, lo:hi], scalar=0.2, in1=placed[t % 2][:, lo:hi],
+                op0=ALU.mult, op1=ALU.add,
+            )
+            nc.sync.dma_start(out=out_rows[:, t, lo:hi], in_=y[:, t, lo:hi])
+
+        y_grouped = keep.tile([P, T, PACK], BF16, name="y_grouped", align_bytes=64)
+        y_codes = keep.tile([P, T], I32, name="y_codes", align_bytes=64)
+        y_scales = keep.tile([P, T], U8, name="y_scales", align_bytes=64)
+        words_out = out_1[0].rearrange("p c r -> p (c r)").bitcast(I32)
+
+        def regroup(copy, lo, hi):
+            copy(
+                out=y_grouped[:, lo:hi, :].rearrange("p (c i) t -> p c t i", i=4),
+                in_=y[:, :, lo:hi].rearrange("p t (c i) -> p c t i", i=4),
+            )
+
+        def quantize_out(lo, hi):
+            nc.vector.quantize_mx(
+                out=y_codes[:, lo:hi].bitcast(FP8X4),
+                scales=y_scales[:, lo:hi],
+                in_=y_grouped[:, lo:hi, :].rearrange("p c t -> p (c t)"),
+            )
+
+        gather(0)
+        deal(wa_dealt[:], wa_raw[:])
+        deal(wa_scale[:], wa_scale_raw[:])
+        first_layer(0)
+        first_layer(1)
+        gather(1)
+        first_layer(2)
+        first_layer(3)
+        block_means(0)
+        block_means(1)
+        centre(0)
+        block_means(2)
+        centre(1)
+        deal(wb_dealt[:].bitcast(U16), wb_raw[:].bitcast(U16))
+        deal(wb_scale[:], wb_scale_raw[:])
+        block_means(3)
+        quantize_hidden(0)
+        second_layer(0)
+        centre(2)
+        centre(3)
+        scatter(0, 0, HALF)
+        quantize_hidden(1)
+        second_layer(1)
+        scatter(1, 0, HALF)
+        scatter(0, HALF, J)
+        scatter(1, HALF, J)
+        add_residual(0, 0, T)
+        scatter(2, 0, J)
+        add_residual(1, 0, T)
+        scatter(3, 0, J)
+        add_residual(2, 0, T)
+        add_residual(3, 0, T // 2)
+        add_residual(3, T // 2, T)
+        regroup(nc.scalar.copy, 0, 256)
+        regroup(nc.vector.tensor_copy, 512, 768)
+        regroup(nc.scalar.copy, 256, 512)
+        regroup(nc.vector.tensor_copy, 768, 1024)
+        quantize_out(0, 256)
+        quantize_out(512, 1024)
+        nc.sync.dma_start(out=words_out[:, 512:1024], in_=y_codes[:, 512:1024])
+        quantize_out(256, 512)
+        nc.sync.dma_start(out=words_out[:, 0:512], in_=y_codes[:, 0:512])
+        for q in range(4):
+            nc.scalar.dma_start(
+                out=out_2[0, 4 * q : 4 * q + 4, :].bitcast(I32), in_=y_scales[32 * q : 32 * q + 4, :].bitcast(I32)
+            )

@@ -1,6 +1,7 @@
 from contextlib import ExitStack
 
 import concourse.mybir as mybir
+from concourse.masks import make_identity
 
 K, T, J, R, N = 512, 1024, 512, 512, 512
 FLOPS = 2 * K * R * J + 2 * R * N * J
@@ -22,7 +23,7 @@ PACK = 4
 RUN = 8
 CHUNK = 128
 HALF = 256
-OUT_CHUNK = 256
+BANK = 512
 
 
 def load_scale_rows(nc, plane, rows):
@@ -47,9 +48,12 @@ def tile_moe_expert_hidden_less_block_mean_pl_kernel(
         nc.vector.memset(x_scale_raw[:].bitcast(I32), 0)
         nc.vector.memset(wa_scale_raw[:].bitcast(I32), 0)
         nc.vector.memset(wb_scale_raw[:].bitcast(I32), 0)
-        placed = [keep.tile([P, T], F32, name=f"placed{u}", align_bytes=64) for u in range(2)]
-        for u in range(2):
-            nc.vector.memset(placed[u][:], 0.0)
+        windows = [keep.tile([P, T], F32, name=f"window{u}", align_bytes=64) for u in range(3)]
+        for u in range(3):
+            nc.vector.memset(windows[u][:].bitcast(I32), 0)
+        placed = [windows[0], windows[1], windows[2], windows[0]]
+        identity = keep.tile([P, P], F32, name="identity")
+        make_identity(nc, identity[:])
 
         x_raw = keep.tile([P, 2 * T], U8, name="x_raw", align_bytes=64)
         wa_raw = keep.tile([P, R], I32, name="wa_raw", align_bytes=64)
@@ -83,7 +87,7 @@ def tile_moe_expert_hidden_less_block_mean_pl_kernel(
                 out=dst.rearrange("p (t m) -> p m t", t=PACK), in_=src.rearrange("p (m t) -> p m t", t=PACK)
             )
 
-        banks = [psum.tile([P, PACK, CHUNK], F32, name=f"a_bank{c}") for c in range(J // CHUNK)]
+        banks = [psum.tile([P, PACK, CHUNK], F32, name=f"a_bank{c}", tag=f"bank{c}") for c in range(J // CHUNK)]
         sums = [keep.tile([P, PACK, CHUNK // RUN], F32, name=f"sums{c}") for c in range(J // CHUNK)]
         means = [keep.tile([P, CHUNK // RUN, PACK], F32, name=f"means{c}") for c in range(J // CHUNK)]
         centred = keep.tile([P, J * PACK], BF16, name="centred", align_bytes=64)
@@ -134,39 +138,64 @@ def tile_moe_expert_hidden_less_block_mean_pl_kernel(
                 in_=hid[:, h * HALF * PACK : (h + 1) * HALF * PACK],
             )
 
-        p_banks = [[psum.tile([P, 2, HALF], F32, name=f"p_bank{h}{u}") for u in range(2)] for h in range(2)]
-        p_sb = [keep.tile([P, 2, J], F32, name=f"p_sb{u}") for u in range(2)]
+        p_sb = [keep.tile([P, J], F32, name=f"p_sb{t}") for t in range(PACK)]
 
-        def second_layer(h):
+        def second_layer(h, rows, tag):
             cols = slice(h * HALF, (h + 1) * HALF)
-            for u in range(2):
-                for e in range(2):
-                    t = 2 * u + e
-                    nc.tensor.matmul_mx(
-                        out=p_banks[h][u][:, e, :],
-                        lhsT=wb_dealt[:, 2 * t * P : 2 * (t + 1) * P].bitcast(FP4X4),
-                        lhsT_scale=wb_scale[:, t * P : (t + 1) * P],
-                        rhs=hid_codes[:, cols].bitcast(FP8X4),
-                        rhs_scale=hid_scales[:, cols],
-                        start=True,
-                        stop=True,
-                    )
-                nc.scalar.copy(out=p_sb[u][:, :, cols], in_=p_banks[h][u][:])
+            bank = psum.tile([P, len(rows), HALF], F32, name=f"p_bank{h}{rows[0]}", tag=tag)
+            for e, t in enumerate(rows):
+                nc.tensor.matmul_mx(
+                    out=bank[:, e, :],
+                    lhsT=wb_dealt[:, 2 * t * P : 2 * (t + 1) * P].bitcast(FP4X4),
+                    lhsT_scale=wb_scale[:, t * P : (t + 1) * P],
+                    rhs=hid_codes[:, cols].bitcast(FP8X4),
+                    rhs_scale=hid_scales[:, cols],
+                    start=True,
+                    stop=True,
+                )
+            for e, t in enumerate(rows):
+                nc.scalar.activation(out=p_sb[t][:, cols], in_=bank[:, e, :], func=ACT.Copy, scale=5.0 if t < 2 else 1.0)
 
         def scatter(t, lo, hi):
-            nc.vector.tensor_copy(
-                placed[t % 2][:].indirect(offsets[:, lo // 16 : hi // 16]), p_sb[t // 2][:, t % 2, lo:hi]
-            )
+            nc.vector.tensor_copy(placed[t][:].indirect(offsets[:, lo // 16 : hi // 16]), p_sb[t][:, lo:hi])
 
-        y = keep.tile([P, PACK, T], F32, name="y")
+        y = [keep.tile([P, PACK, BANK], F32, name=f"y{b}") for b in range(T // BANK)]
         out_rows = out_0.rearrange("(p t) c -> p t c", t=PACK)
 
-        def add_residual(t, lo, hi):
+        def add_residual(t, b):
+            cols = slice(b * BANK, (b + 1) * BANK)
             nc.vector.scalar_tensor_tensor(
-                out=y[:, t, lo:hi], in0=res_sb[t][:, lo:hi], scalar=0.2, in1=placed[t % 2][:, lo:hi],
+                out=y[b][:, t, :], in0=res_sb[t][:, cols], scalar=0.2, in1=placed[t][:, cols],
                 op0=ALU.mult, op1=ALU.add,
             )
-            nc.sync.dma_start(out=out_rows[:, t, lo:hi], in_=y[:, t, lo:hi])
+            nc.sync.dma_start(out=out_rows[:, t, cols], in_=y[b][:, t, :])
+
+        sum_banks = {
+            (t, b): psum.tile([P, BANK], F32, name=f"sum_bank{t}{b}") for t in range(2) for b in range(T // BANK)
+        }
+        turned = {(t, b): keep.tile([P, BANK], F32, name=f"turned{t}{b}") for t in range(2) for b in range(T // BANK)}
+
+        def turn(bank, src, first, last):
+            for k in range(BANK // P):
+                block = slice(k * P, (k + 1) * P)
+                nc.tensor.matmul(
+                    out=bank[:, block], lhsT=src[:, block], rhs=identity[:], is_transpose=True,
+                    start=first and k == 0, stop=last and k == BANK // P - 1,
+                )
+
+        def open_sum(t, b):
+            turn(sum_banks[t, b], res_sb[t][:, b * BANK : (b + 1) * BANK], True, False)
+
+        def close_sum(t, b):
+            turn(sum_banks[t, b], placed[t][:, b * BANK : (b + 1) * BANK], False, True)
+            nc.scalar.activation(out=turned[t, b][:], in_=sum_banks[t, b][:], func=ACT.Copy, scale=0.2)
+
+        def turn_back(t, b, tag):
+            cols = slice(b * BANK, (b + 1) * BANK)
+            bank = psum.tile([P, BANK], F32, name=f"y_bank{t}{b}", tag=tag)
+            turn(bank, turned[t, b][:], True, True)
+            nc.scalar.copy(out=y[b][:, t, :], in_=bank[:])
+            nc.scalar.dma_start(out=out_rows[:, t, cols], in_=y[b][:, t, :])
 
         y_grouped = keep.tile([P, T, PACK], BF16, name="y_grouped", align_bytes=64)
         y_codes = keep.tile([P, T], I32, name="y_codes", align_bytes=64)
@@ -176,7 +205,7 @@ def tile_moe_expert_hidden_less_block_mean_pl_kernel(
         def regroup(copy, lo, hi):
             copy(
                 out=y_grouped[:, lo:hi, :].rearrange("p (c i) t -> p c t i", i=4),
-                in_=y[:, :, lo:hi].rearrange("p t (c i) -> p c t i", i=4),
+                in_=y[lo // BANK][:, :, lo % BANK : lo % BANK + hi - lo].rearrange("p t (c i) -> p c t i", i=4),
             )
 
         def quantize_out(lo, hi):
@@ -194,40 +223,53 @@ def tile_moe_expert_hidden_less_block_mean_pl_kernel(
         gather(1)
         first_layer(2)
         first_layer(3)
+        deal(wb_scale[:], wb_scale_raw[:])
+        deal(wb_dealt[:].bitcast(U16), wb_raw[:].bitcast(U16))
+        for t in range(2):
+            for b in range(T // BANK):
+                open_sum(t, b)
         block_means(0)
         block_means(1)
         centre(0)
         block_means(2)
         centre(1)
-        deal(wb_dealt[:].bitcast(U16), wb_raw[:].bitcast(U16))
-        deal(wb_scale[:], wb_scale_raw[:])
         block_means(3)
         quantize_hidden(0)
-        second_layer(0)
+        second_layer(0, (0, 1), "bank0")
+        second_layer(0, (2, 3), "bank1")
         centre(2)
         centre(3)
         scatter(0, 0, HALF)
         quantize_hidden(1)
-        second_layer(1)
+        second_layer(1, (0,), "bank2")
+        second_layer(1, (2,), "bank3")
+        second_layer(1, (1,), "bank0")
+        second_layer(1, (3,), "bank1")
         scatter(1, 0, HALF)
+        scatter(2, 0, HALF)
         scatter(0, HALF, J)
+        close_sum(0, 0)
+        close_sum(0, 1)
+        scatter(2, HALF, J)
         scatter(1, HALF, J)
-        add_residual(0, 0, T)
-        scatter(2, 0, J)
-        add_residual(1, 0, T)
+        turn_back(0, 0, "bank2")
+        close_sum(1, 0)
+        turn_back(0, 1, "bank3")
+        close_sum(1, 1)
+        turn_back(1, 0, "bank0")
+        turn_back(1, 1, "bank1")
+        add_residual(2, 0)
         scatter(3, 0, J)
-        add_residual(2, 0, T)
-        add_residual(3, 0, T // 2)
-        add_residual(3, T // 2, T)
-        regroup(nc.scalar.copy, 0, 256)
-        regroup(nc.vector.tensor_copy, 512, 768)
-        regroup(nc.scalar.copy, 256, 512)
-        regroup(nc.vector.tensor_copy, 768, 1024)
-        quantize_out(0, 256)
-        quantize_out(512, 1024)
-        nc.sync.dma_start(out=words_out[:, 512:1024], in_=y_codes[:, 512:1024])
-        quantize_out(256, 512)
-        nc.sync.dma_start(out=words_out[:, 0:512], in_=y_codes[:, 0:512])
+        add_residual(2, 1)
+        add_residual(3, 0)
+        add_residual(3, 1)
+        regroup(nc.vector.tensor_copy, 0, 512)
+        regroup(nc.scalar.copy, 512, 768)
+        regroup(nc.scalar.copy, 768, 896)
+        regroup(nc.vector.tensor_copy, 896, 1024)
+        for lo, hi in ((0, 512), (512, 768), (768, 1024)):
+            quantize_out(lo, hi)
+            nc.sync.dma_start(out=words_out[:, lo:hi], in_=y_codes[:, lo:hi])
         for q in range(4):
             nc.scalar.dma_start(
                 out=out_2[0, 4 * q : 4 * q + 4, :].bitcast(I32), in_=y_scales[32 * q : 32 * q + 4, :].bitcast(I32)

@@ -45,9 +45,9 @@ def tile_moe_expert_hidden_less_block_mean_pl_kernel(
         x_scale_raw = keep.tile([P, T], U8, name="x_scale_raw", align_bytes=64)
         wa_scale_raw = keep.tile([P, R], U8, name="wa_scale_raw", align_bytes=64)
         wb_scale_raw = keep.tile([P, N], U8, name="wb_scale_raw", align_bytes=64)
-        nc.vector.memset(x_scale_raw[:].bitcast(I32), 0)
-        nc.vector.memset(wa_scale_raw[:].bitcast(I32), 0)
-        nc.vector.memset(wb_scale_raw[:].bitcast(I32), 0)
+        nc.gpsimd.memset(x_scale_raw[:].bitcast(I32), 0)
+        nc.gpsimd.memset(wa_scale_raw[:].bitcast(I32), 0)
+        nc.gpsimd.memset(wb_scale_raw[:].bitcast(I32), 0)
         windows = [keep.tile([P, T], F32, name=f"window{u}", align_bytes=64) for u in range(3)]
         for u in range(3):
             nc.vector.memset(windows[u][:].bitcast(I32), 0)
@@ -154,7 +154,7 @@ def tile_moe_expert_hidden_less_block_mean_pl_kernel(
                     stop=True,
                 )
             for e, t in enumerate(rows):
-                nc.scalar.activation(out=p_sb[t][:, cols], in_=bank[:, e, :], func=ACT.Copy, scale=5.0 if t < 2 else 1.0)
+                nc.scalar.activation(out=p_sb[t][:, cols], in_=bank[:, e, :], func=ACT.Copy, scale=5.0 if t == 0 else 1.0)
 
         def scatter(t, lo, hi):
             nc.vector.tensor_copy(placed[t][:].indirect(offsets[:, lo // 16 : hi // 16]), p_sb[t][:, lo:hi])
@@ -171,9 +171,9 @@ def tile_moe_expert_hidden_less_block_mean_pl_kernel(
             nc.sync.dma_start(out=out_rows[:, t, cols], in_=y[b][:, t, :])
 
         sum_banks = {
-            (t, b): psum.tile([P, BANK], F32, name=f"sum_bank{t}{b}") for t in range(2) for b in range(T // BANK)
+            (t, b): psum.tile([P, BANK], F32, name=f"sum_bank{t}{b}") for t in range(1) for b in range(T // BANK)
         }
-        turned = {(t, b): keep.tile([P, BANK], F32, name=f"turned{t}{b}") for t in range(2) for b in range(T // BANK)}
+        turned = {(t, b): keep.tile([P, BANK], F32, name=f"turned{t}{b}") for t in range(1) for b in range(T // BANK)}
 
         def turn(bank, src, first, last):
             for k in range(BANK // P):
@@ -190,9 +190,9 @@ def tile_moe_expert_hidden_less_block_mean_pl_kernel(
             turn(sum_banks[t, b], placed[t][:, b * BANK : (b + 1) * BANK], False, True)
             nc.scalar.activation(out=turned[t, b][:], in_=sum_banks[t, b][:], func=ACT.Copy, scale=0.2)
 
-        def turn_back(t, b, tag):
+        def turn_back(t, b):
             cols = slice(b * BANK, (b + 1) * BANK)
-            bank = psum.tile([P, BANK], F32, name=f"y_bank{t}{b}", tag=tag)
+            bank = psum.tile([P, BANK], F32, name=f"y_bank{t}{b}")
             turn(bank, turned[t, b][:], True, True)
             nc.scalar.copy(out=y[b][:, t, :], in_=bank[:])
             nc.scalar.dma_start(out=out_rows[:, t, cols], in_=y[b][:, t, :])
@@ -214,6 +214,7 @@ def tile_moe_expert_hidden_less_block_mean_pl_kernel(
                 scales=y_scales[:, lo:hi],
                 in_=y_grouped[:, lo:hi, :].rearrange("p c t -> p (c t)"),
             )
+            nc.sync.dma_start(out=words_out[:, lo:hi], in_=y_codes[:, lo:hi])
 
         gather(0)
         deal(wa_dealt[:], wa_raw[:])
@@ -225,9 +226,8 @@ def tile_moe_expert_hidden_less_block_mean_pl_kernel(
         first_layer(3)
         deal(wb_scale[:], wb_scale_raw[:])
         deal(wb_dealt[:].bitcast(U16), wb_raw[:].bitcast(U16))
-        for t in range(2):
-            for b in range(T // BANK):
-                open_sum(t, b)
+        for b in range(T // BANK):
+            open_sum(0, b)
         block_means(0)
         block_means(1)
         centre(0)
@@ -242,35 +242,34 @@ def tile_moe_expert_hidden_less_block_mean_pl_kernel(
         scatter(0, 0, HALF)
         quantize_hidden(1)
         second_layer(1, (0,), "bank2")
-        second_layer(1, (2,), "bank3")
-        second_layer(1, (1,), "bank0")
+        second_layer(1, (1,), "bank3")
+        second_layer(1, (2,), "bank0")
         second_layer(1, (3,), "bank1")
         scatter(1, 0, HALF)
         scatter(2, 0, HALF)
         scatter(0, HALF, J)
         close_sum(0, 0)
         close_sum(0, 1)
-        scatter(2, HALF, J)
+        turn_back(0, 0)
+        turn_back(0, 1)
         scatter(1, HALF, J)
-        turn_back(0, 0, "bank2")
-        close_sum(1, 0)
-        turn_back(0, 1, "bank3")
-        close_sum(1, 1)
-        turn_back(1, 0, "bank0")
-        turn_back(1, 1, "bank1")
-        add_residual(2, 0)
+        scatter(2, HALF, J)
+        add_residual(1, 0)
+        add_residual(1, 1)
         scatter(3, 0, J)
-        add_residual(2, 1)
-        add_residual(3, 0)
-        add_residual(3, 1)
-        regroup(nc.vector.tensor_copy, 0, 512)
-        regroup(nc.scalar.copy, 512, 768)
-        regroup(nc.scalar.copy, 768, 896)
-        regroup(nc.vector.tensor_copy, 896, 1024)
-        for lo, hi in ((0, 512), (512, 768), (768, 1024)):
-            quantize_out(lo, hi)
-            nc.sync.dma_start(out=words_out[:, lo:hi], in_=y_codes[:, lo:hi])
+        for b in range(T // BANK):
+            add_residual(2, b)
+            add_residual(3, b)
+        regroup(nc.scalar.copy, 0, 256)
+        regroup(nc.scalar.copy, 256, 512)
+        regroup(nc.scalar.copy, 512, 640)
+        quantize_out(0, 256)
+        regroup(nc.vector.tensor_copy, 640, 1024)
+        quantize_out(256, 512)
+        quantize_out(768, 1024)
+        quantize_out(512, 768)
         for q in range(4):
-            nc.scalar.dma_start(
+            queue = nc.sync if q % 2 else nc.scalar
+            queue.dma_start(
                 out=out_2[0, 4 * q : 4 * q + 4, :].bitcast(I32), in_=y_scales[32 * q : 32 * q + 4, :].bitcast(I32)
             )

from contextlib import ExitStack

import concourse.mybir as mybir
from concourse.masks import make_identity

K, T, J, R, N = 512, 1024, 512, 512, 512
FLOPS = 2 * K * R * J + 2 * R * N * J

F32 = mybir.dt.float32
BF16 = mybir.dt.bfloat16
I32 = mybir.dt.int32
U32 = mybir.dt.uint32
U16 = mybir.dt.uint16
U8 = mybir.dt.uint8
FP8X4 = mybir.dt.float8_e4m3fn_x4
FP4X4 = mybir.dt.float4_e2m1fn_x4
ALU = mybir.AluOpType
ACT = mybir.ActivationFunctionType
AXIS_X = mybir.AxisListType.X

P = 128
PACK = 4
RUN = 8
CHUNK = 128
HALF = 256
BANK = 512


def load_scale_rows(nc, plane, rows):
    for q in range(4):
        nc.sync.dma_start(out=plane[32 * q : 32 * q + 4, :].bitcast(I32), in_=rows[4 * q : 4 * q + 4, :].bitcast(I32))


def tile_moe_expert_hidden_less_block_mean_pl_kernel(
    tc, xt_words, xt_scales, wa_words, wa_scales, wb_words, wb_scales, res, offs, out_0, out_1, out_2
):
    nc = tc.nc
    with ExitStack() as ctx:
        keep = ctx.enter_context(tc.tile_pool(name="keep", bufs=1))
        psum = ctx.enter_context(tc.psum_pool(name="psum", bufs=1))

        offsets = keep.tile([P, J // 16], U16, name="offsets")
        nc.sync.dma_start(offsets[:], offs)

        x_scale_raw = keep.tile([P, T], U8, name="x_scale_raw", align_bytes=64)
        wa_scale_raw = keep.tile([P, R], U8, name="wa_scale_raw", align_bytes=64)
        wb_scale_raw = keep.tile([P, N], U8, name="wb_scale_raw", align_bytes=64)
        nc.gpsimd.memset(x_scale_raw[:].bitcast(I32), 0)
        nc.gpsimd.memset(wa_scale_raw[:].bitcast(I32), 0)
        nc.gpsimd.memset(wb_scale_raw[:].bitcast(I32), 0)
        windows = [keep.tile([P, T], F32, name=f"window{u}", align_bytes=64) for u in range(3)]
        for u in range(3):
            nc.vector.memset(windows[u][:].bitcast(I32), 0)
        placed = [windows[0], windows[1], windows[2], windows[0]]
        identity = keep.tile([P, P], F32, name="identity")
        make_identity(nc, identity[:])

        x_raw = keep.tile([P, 2 * T], U8, name="x_raw", align_bytes=64)
        wa_raw = keep.tile([P, R], I32, name="wa_raw", align_bytes=64)
        wb_raw = keep.tile([P, 2 * N], U8, name="wb_raw", align_bytes=64)
        nc.sync.dma_start(out=x_raw[:].bitcast(I32), in_=xt_words[0].bitcast(I32))
        load_scale_rows(nc, x_scale_raw, xt_scales[0])
        nc.sync.dma_start(out=wa_raw[:], in_=wa_words[0].rearrange("p c r -> p (c r)").bitcast(I32))
        load_scale_rows(nc, wa_scale_raw, wa_scales[0])
        nc.sync.dma_start(out=wb_raw[:].bitcast(I32), in_=wb_words[0].bitcast(I32))
        load_scale_rows(nc, wb_scale_raw, wb_scales[0])
        res_rows = res.rearrange("(p t) c -> p t c", t=PACK)
        res_sb = [keep.tile([P, T], F32, name=f"res{t}") for t in range(PACK)]
        for t in range(PACK):
            nc.sync.dma_start(out=res_sb[t][:], in_=res_rows[:, t, :])

        x_words = keep.tile([P, 2 * J], U8, name="x_words", align_bytes=64)
        x_scales = keep.tile([P, J], U8, name="x_scales", align_bytes=64)
        wa_dealt = keep.tile([P, R], I32, name="wa_dealt", align_bytes=64)
        wa_scale = keep.tile([P, R], U8, name="wa_scale", align_bytes=64)
        wb_dealt = keep.tile([P, 2 * N], U8, name="wb_dealt", align_bytes=64)
        wb_scale = keep.tile([P, N], U8, name="wb_scale", align_bytes=64)

        def gather(h):
            cols = slice(h * HALF, (h + 1) * HALF)
            listed = offsets[:, h * HALF // 16 : (h + 1) * HALF // 16]
            nc.vector.tensor_copy(x_words[:].bitcast(U16)[:, cols], x_raw[:].bitcast(U16).indirect(listed))
            nc.vector.tensor_copy(x_scales[:, cols], x_scale_raw[:].indirect(listed))

        def deal(dst, src):
            nc.vector.tensor_copy(
                out=dst.rearrange("p (t m) -> p m t", t=PACK), in_=src.rearrange("p (m t) -> p m t", t=PACK)
            )

        banks = [psum.tile([P, PACK, CHUNK], F32, name=f"a_bank{c}", tag=f"bank{c}") for c in range(J // CHUNK)]
        sums = [keep.tile([P, PACK, CHUNK // RUN], F32, name=f"sums{c}") for c in range(J // CHUNK)]
        means = [keep.tile([P, CHUNK // RUN, PACK], F32, name=f"means{c}") for c in range(J // CHUNK)]
        centred = keep.tile([P, J * PACK], BF16, name="centred", align_bytes=64)
        hid = keep.tile([P, J * PACK], BF16, name="hid", align_bytes=64)
        hid_codes = keep.tile([P, J], U32, name="hid_codes", align_bytes=64)
        hid_scales = keep.tile([P, J], U8, name="hid_scales", align_bytes=64)

        def first_layer(c):
            cols = slice(c * CHUNK, (c + 1) * CHUNK)
            for t in range(PACK):
                w_cols = slice(t * P, (t + 1) * P)
                nc.tensor.matmul_mx(
                    out=banks[c][:, t, :],
                    lhsT=wa_dealt[:, w_cols].bitcast(FP8X4),
                    lhsT_scale=wa_scale[:, w_cols],
                    rhs=x_words[:, 2 * c * CHUNK : 2 * (c + 1) * CHUNK].bitcast(FP4X4),
                    rhs_scale=x_scales[:, cols],
                    start=True,
                    stop=True,
                )

        def block_means(c):
            nc.vector.tensor_reduce(
                out=sums[c][:].rearrange("p t b -> p (t b)"),
                in_=banks[c][:].rearrange("p t (b i) -> p (t b) i", i=RUN),
                axis=AXIS_X,
                op=ALU.add,
            )
            nc.scalar.activation(
                out=means[c][:], in_=sums[c][:].rearrange("p t b -> p b t"), func=ACT.Copy, scale=1.0 / RUN
            )

        def centre(c):
            cols = slice(c * CHUNK * PACK, (c + 1) * CHUNK * PACK)
            nc.vector.tensor_tensor(
                out=centred[:, cols].rearrange("p (b i t) -> p b i t", i=RUN, t=PACK),
                in0=banks[c][:].rearrange("p t (b i) -> p b i t", i=RUN),
                in1=means[c][:].rearrange("p b (o t) -> p b o t", o=1).to_broadcast([P, CHUNK // RUN, RUN, PACK]),
                op=ALU.subtract,
            )
            nc.scalar.activation(out=hid[:, cols], in_=centred[:, cols], func=ACT.Relu)

        def quantize_hidden(h):
            cols = slice(h * HALF, (h + 1) * HALF)
            nc.vector.quantize_mx(
                out=hid_codes[:, cols].bitcast(FP8X4),
                scales=hid_scales[:, cols],
                in_=hid[:, h * HALF * PACK : (h + 1) * HALF * PACK],
            )

        p_sb = [keep.tile([P, J], F32, name=f"p_sb{t}") for t in range(PACK)]

        def second_layer(h, rows, tag):
            cols = slice(h * HALF, (h + 1) * HALF)
            bank = psum.tile([P, len(rows), HALF], F32, name=f"p_bank{h}{rows[0]}", tag=tag)
            for e, t in enumerate(rows):
                nc.tensor.matmul_mx(
                    out=bank[:, e, :],
                    lhsT=wb_dealt[:, 2 * t * P : 2 * (t + 1) * P].bitcast(FP4X4),
                    lhsT_scale=wb_scale[:, t * P : (t + 1) * P],
                    rhs=hid_codes[:, cols].bitcast(FP8X4),
                    rhs_scale=hid_scales[:, cols],
                    start=True,
                    stop=True,
                )
            for e, t in enumerate(rows):
                nc.scalar.activation(out=p_sb[t][:, cols], in_=bank[:, e, :], func=ACT.Copy, scale=5.0 if t == 0 else 1.0)

        def scatter(t, lo, hi):
            nc.vector.tensor_copy(placed[t][:].indirect(offsets[:, lo // 16 : hi // 16]), p_sb[t][:, lo:hi])

        y = [keep.tile([P, PACK, BANK], F32, name=f"y{b}") for b in range(T // BANK)]
        out_rows = out_0.rearrange("(p t) c -> p t c", t=PACK)

        def add_residual(t, b):
            cols = slice(b * BANK, (b + 1) * BANK)
            nc.vector.scalar_tensor_tensor(
                out=y[b][:, t, :], in0=res_sb[t][:, cols], scalar=0.2, in1=placed[t][:, cols],
                op0=ALU.mult, op1=ALU.add,
            )
            nc.sync.dma_start(out=out_rows[:, t, cols], in_=y[b][:, t, :])

        sum_banks = {
            (t, b): psum.tile([P, BANK], F32, name=f"sum_bank{t}{b}") for t in range(1) for b in range(T // BANK)
        }
        turned = {(t, b): keep.tile([P, BANK], F32, name=f"turned{t}{b}") for t in range(1) for b in range(T // BANK)}

        def turn(bank, src, first, last):
            for k in range(BANK // P):
                block = slice(k * P, (k + 1) * P)
                nc.tensor.matmul(
                    out=bank[:, block], lhsT=src[:, block], rhs=identity[:], is_transpose=True,
                    start=first and k == 0, stop=last and k == BANK // P - 1,
                )

        def open_sum(t, b):
            turn(sum_banks[t, b], res_sb[t][:, b * BANK : (b + 1) * BANK], True, False)

        def close_sum(t, b):
            turn(sum_banks[t, b], placed[t][:, b * BANK : (b + 1) * BANK], False, True)
            nc.scalar.activation(out=turned[t, b][:], in_=sum_banks[t, b][:], func=ACT.Copy, scale=0.2)

        def turn_back(t, b):
            cols = slice(b * BANK, (b + 1) * BANK)
            bank = psum.tile([P, BANK], F32, name=f"y_bank{t}{b}")
            turn(bank, turned[t, b][:], True, True)
            nc.scalar.copy(out=y[b][:, t, :], in_=bank[:])
            nc.scalar.dma_start(out=out_rows[:, t, cols], in_=y[b][:, t, :])

        y_grouped = keep.tile([P, T, PACK], BF16, name="y_grouped", align_bytes=64)
        y_codes = keep.tile([P, T], I32, name="y_codes", align_bytes=64)
        y_scales = keep.tile([P, T], U8, name="y_scales", align_bytes=64)
        words_out = out_1[0].rearrange("p c r -> p (c r)").bitcast(I32)

        def regroup(copy, lo, hi):
            copy(
                out=y_grouped[:, lo:hi, :].rearrange("p (c i) t -> p c t i", i=4),
                in_=y[lo // BANK][:, :, lo % BANK : lo % BANK + hi - lo].rearrange("p t (c i) -> p c t i", i=4),
            )

        def quantize_out(lo, hi):
            nc.vector.quantize_mx(
                out=y_codes[:, lo:hi].bitcast(FP8X4),
                scales=y_scales[:, lo:hi],
                in_=y_grouped[:, lo:hi, :].rearrange("p c t -> p (c t)"),
            )
            nc.sync.dma_start(out=words_out[:, lo:hi], in_=y_codes[:, lo:hi])

        gather(0)
        deal(wa_dealt[:], wa_raw[:])
        deal(wa_scale[:], wa_scale_raw[:])
        first_layer(0)
        first_layer(1)
        gather(1)
        first_layer(2)
        first_layer(3)
        deal(wb_scale[:], wb_scale_raw[:])
        deal(wb_dealt[:].bitcast(U16), wb_raw[:].bitcast(U16))
        for b in range(T // BANK):
            open_sum(0, b)
        block_means(0)
        block_means(1)
        centre(0)
        block_means(2)
        centre(1)
        block_means(3)
        quantize_hidden(0)
        second_layer(0, (0, 1), "bank0")
        second_layer(0, (2, 3), "bank1")
        centre(2)
        centre(3)
        scatter(0, 0, HALF)
        quantize_hidden(1)
        second_layer(1, (0,), "bank2")
        second_layer(1, (1,), "bank3")
        second_layer(1, (2,), "bank0")
        second_layer(1, (3,), "bank1")
        scatter(1, 0, HALF)
        scatter(2, 0, HALF)
        scatter(0, HALF, J)
        close_sum(0, 0)
        close_sum(0, 1)
        turn_back(0, 0)
        turn_back(0, 1)
        scatter(1, HALF, J)
        scatter(2, HALF, J)
        add_residual(1, 0)
        add_residual(1, 1)
        scatter(3, 0, J)
        for b in range(T // BANK):
            add_residual(2, b)
            add_residual(3, b)
        regroup(nc.scalar.copy, 0, 256)
        regroup(nc.scalar.copy, 256, 512)
        regroup(nc.scalar.copy, 512, 640)
        quantize_out(0, 256)
        regroup(nc.vector.tensor_copy, 640, 1024)
        quantize_out(256, 512)
        quantize_out(768, 1024)
        quantize_out(512, 768)
        for q in range(4):
            queue = nc.sync if q % 2 else nc.scalar
            queue.dma_start(
                out=out_2[0, 4 * q : 4 * q + 4, :].bitcast(I32), in_=y_scales[32 * q : 32 * q + 4, :].bitcast(I32)
            )
